import numpy as np
import ml_dtypes


def mxq(x, axis, fmt="e4m3"):
    dtype, down = {"e4m3": (ml_dtypes.float8_e4m3fn, 7), "e5m2": (ml_dtypes.float8_e5m2, 14)}[fmt]
    v = np.moveaxis(np.asarray(x, np.float32).astype(ml_dtypes.bfloat16).astype(np.float64), axis, -1)
    blocks = v.reshape(v.shape[:-1] + (-1, 32))
    amax = np.abs(blocks).max(-1, keepdims=True)
    byte = np.maximum(np.where(amax > 0, np.frexp(amax)[1] - 1 + 127, 0) - down, 1)
    scale = np.exp2(byte - 127.0)
    codes = (blocks / scale).astype(np.float32).astype(dtype).astype(np.float64)
    return np.moveaxis((codes * scale).reshape(v.shape), -1, axis)


WIDE = False


def mx_kscale(k):
    if not WIDE:
        return np.ones(k)
    levels = np.array([10, -10, 5, -5, 0])
    if k % 512:
        return np.exp2(np.random.permutation(np.resize(levels, k // 32))).repeat(32)
    a = np.empty((k // 512, 16))
    for p in range(k // 512):
        a[p, :8] = np.random.permutation(np.resize(levels, 8))
        for g in range(8):
            far = levels[np.abs(levels - a[p, g]) >= 10]
            a[p, g + 8] = far[np.random.randint(len(far))]
    return np.exp2(a.ravel()).repeat(32)


def f64(x):
    return np.asarray(x).astype(np.float64)


def striped(idx):
    return np.tile(np.asarray(idx).reshape(-1, 16).T, (8, 1)).astype(np.uint16)


def unstriped(offs):
    return offs[:16].T.reshape(-1).astype(np.int64)


E2M1 = np.array([0.0, 0.5, 1.0, 1.5, 2.0, 3.0, 4.0, 6.0, -0.0, -0.5, -1.0, -1.5, -2.0, -3.0, -4.0, -6.0])


def pack_weight(w, fmt):
    k, n = w.shape
    w = f64(np.asarray(w, np.float32).astype(ml_dtypes.bfloat16)).reshape(k // 32, 32, n)
    amax = np.abs(w).max(1)
    if fmt == "e4m3":
        byte = np.frexp(amax)[1] - 1 + 127 - 7
    else:
        mant, ex = np.frexp(amax / 6.0)
        byte = np.where(mant > 0.5, ex, ex - 1) + 127
    byte = np.clip(np.where(amax > 0, byte, 1), 1, 254)
    scaled = (w * np.exp2(127.0 - byte)[:, None, :]).reshape(k, n).astype(np.float32)
    by_word = np.ascontiguousarray(scaled.reshape(k // 512, 128, 4, n).transpose(0, 1, 3, 2))
    if fmt == "e4m3":
        words = by_word.astype(ml_dtypes.float8_e4m3fn).view(np.uint8)
    else:
        c = by_word.astype(ml_dtypes.float4_e2m1fn).view(np.uint8) & 0xF
        words = (c[..., 0::2] | (c[..., 1::2] << 4)).reshape(k // 512, 128, 2 * n)
    return np.ascontiguousarray(words), np.ascontiguousarray(byte.astype(np.uint8).reshape(k // 512, 16, n))


def unpack_weight(words, scales, fmt):
    g, _, n = scales.shape
    words = np.ascontiguousarray(words).reshape(g, 128, n, -1)
    if fmt == "e4m3":
        vals = words.view(ml_dtypes.float8_e4m3fn).astype(np.float64)
    else:
        nib = np.empty((g, 128, n, 4), np.uint8)
        nib[..., 0::2] = words & 0xF
        nib[..., 1::2] = words >> 4
        vals = E2M1[nib]
    vals = vals * np.repeat(np.exp2(scales.astype(np.float64) - 127.0), 8, axis=1)[..., None]
    return vals.transpose(0, 1, 3, 2).reshape(g * 512, n)


def sigmoid(v):
    return 1.0 / (1.0 + np.exp(-v))


D, E, T, I, Q, G = 512, 512, 2048, 512, 256, 32


def setup_inputs():
    n = np.random.standard_normal
    idx = np.random.permutation(T)[:I]
    fd = mx_kscale(D)
    fe = mx_kscale(E)
    keysp = pack_weight(n((D, T)) / fd[:, None], "e4m3")
    valsp = pack_weight(n((E, T)) / fe[:, None], "e4m3")
    return {
        "query": (n((D, Q)) * 1.0 / np.sqrt(D) * fd[:, None]).astype(np.float32),
        "keys_words": keysp[0],
        "keys_scales": keysp[1],
        "steep": (np.random.uniform(1.0, 4.0, (I, 1))).astype(np.float32),
        "fs": (np.random.uniform(1.0, 4.0, (I, 1))).astype(np.float32),
        "gout": (n((E, Q)) * 1 / np.sqrt(E) * fe[:, None]).astype(np.float32),
        "vals_words": valsp[0],
        "vals_scales": valsp[1],
        "offs": striped(idx),
    }


def reference(query, keys_words, keys_scales, steep, fs, gout, vals_words, vals_scales, offs):
    idx = unstriped(offs)
    keysu = unpack_weight(keys_words, keys_scales, "e4m3")
    valsu = unpack_weight(vals_words, vals_scales, "e4m3")
    keysidxg = keysu[:, idx]
    queryq = mxq(f64(query), 0, "e4m3")
    a = keysidxg.T @ queryq
    b = a.reshape(I, G, Q // G).mean(axis=2)
    br = np.repeat(b, Q // G, axis=1)
    w = sigmoid((a - br) * f64(steep))
    valsidxg = valsu[:, idx]
    goutq = mxq(f64(gout), 0, "e4m3")
    dp = valsidxg.T @ goutq
    dz = dp * w * (1.0 - w) * f64(steep) * f64(fs)
    dm = dz.reshape(I, G, Q // G).mean(axis=2)
    dr = np.repeat(dm, Q // G, axis=1)
    y = dz - dr
    return y

@@ -1,0 +1,163 @@
+from contextlib import ExitStack
+
+import concourse.mybir as mybir
+from concourse.masks import make_identity
+
+D, E, T, I, Q, G = 512, 512, 2048, 512, 256, 32
+FLOPS = 2 * I * Q * (D + E)
+
+F32 = mybir.dt.float32
+BF16 = mybir.dt.bfloat16
+I32 = mybir.dt.int32
+U32 = mybir.dt.uint32
+U16 = mybir.dt.uint16
+U8 = mybir.dt.uint8
+FP8X4 = mybir.dt.float8_e4m3fn_x4
+ALU = mybir.AluOpType
+ACT = mybir.ActivationFunctionType
+AX = mybir.AxisListType
+
+P = 128
+PACK = 4
+TILES = I // P
+TEAM = Q // G
+LIST_COLS = P // 16
+STAGE_STEP = 8
+STAGE_FIRST = 4
+
+
+def tile_attend_gteamcontrast_kernel(tc, query, keys_words, keys_scales, steep, fs, gout, vals_words, vals_scales, offs, out):
+    nc = tc.nc
+    with ExitStack() as ctx:
+        sb = ctx.enter_context(tc.tile_pool(name="sb", bufs=1))
+        placed = ctx.enter_context(tc.tile_pool(name="placed", bufs=1))
+        ps = ctx.enter_context(tc.psum_pool(name="ps", bufs=1))
+
+        offsets = sb.tile([P, I // 16], U16, name="offsets")
+        nc.sync.dma_start(offsets[:], offs)
+
+        def load_rows(name, rows):
+            raw = sb.tile([P, PACK, Q], F32, name=name)
+            nc.sync.dma_start(raw[:], rows.rearrange("(p j) q -> p j q", j=PACK))
+            return raw
+
+        def load_words(window, words):
+            nc.sync.dma_start(window[:].bitcast(I32), words[0].rearrange("p n t -> p (n t)").bitcast(I32))
+
+        keys_scale_window = placed.tile([P, T], U8, name="keys_scale_window", align_bytes=64, offset=0)
+        nc.vector.memset(keys_scale_window[:].bitcast(I32), 0)
+        for quad in range(4):
+            nc.scalar.dma_start(
+                keys_scale_window[32 * quad : 32 * quad + 4, :].bitcast(I32),
+                keys_scales[0, 4 * quad : 4 * quad + 4, :].bitcast(I32),
+            )
+        vals_scale_window = sb.tile([P, T], U8, name="vals_scale_window", tag="vals_scale_window", align_bytes=64)
+        nc.vector.memset(vals_scale_window[:].bitcast(I32), 0)
+        nc.scalar.dma_start(vals_scale_window[STAGE_FIRST:P:STAGE_STEP, :].bitcast(I32), vals_scales[0].bitcast(I32))
+
+        query_raw = load_rows("query_raw", query)
+        keys_window = sb.tile([P, T], U32, name="keys_window", align_bytes=64)
+        load_words(keys_window, keys_words)
+        gout_raw = load_rows("gout_raw", gout)
+
+        slot_rows = sb.tile([P, P], F32, name="slot_rows", tag="gout_bf", align_bytes=64)
+        nc.gpsimd.memset(slot_rows[:], 0.0)
+        nc.gpsimd.dma_start(slot_rows[0:TILES, :], steep.rearrange("(t p) o -> t (p o)", p=P))
+        nc.gpsimd.dma_start(slot_rows[TILES : 2 * TILES, :], fs.rearrange("(t p) o -> t (p o)", p=P))
+        identity = sb.tile([P, P], F32, name="identity")
+        make_identity(nc, identity[:])
+        vals_plane = sb.tile([P, I], U8, name="vals_plane", align_bytes=64)
+        nc.gpsimd.memset(vals_plane[:].bitcast(I32), 0)
+
+        def round_and_interleave(name, raw):
+            grouped = sb.tile([P, Q * PACK], BF16, name=name, tag=name, align_bytes=64)
+            nc.scalar.copy(
+                grouped[:].rearrange("p (c i j) -> p c j i", i=4, j=PACK),
+                raw[:].rearrange("p j (c i) -> p c j i", i=4),
+            )
+            return grouped
+
+        def quantise(name, codes, grouped):
+            plane = sb.tile([P, Q], U8, name=name, align_bytes=64)
+            nc.vector.quantize_mx(out=codes[:].bitcast(FP8X4), scales=plane[:], in_=grouped[:])
+            return plane
+
+        def gather_words(picked, window, t):
+            part = picked[:, t * P : (t + 1) * P]
+            nc.vector.tensor_copy(part, window[:].indirect(offsets[:, t * LIST_COLS : (t + 1) * LIST_COLS]))
+            return part
+
+        def by_team(ap):
+            return ap.rearrange("p (g j) -> p g j", j=TEAM)
+
+        def over_team(ap):
+            return ap.unsqueeze(2).to_broadcast([P, G, TEAM])
+
+        keys_plane = sb.tile([P, I], U8, name="keys_plane", align_bytes=64)
+        nc.vector.tensor_copy(keys_plane[:], keys_scale_window[:].indirect(offsets[:]))
+        vals_window = placed.tile([P, T], U32, name="vals_window", align_bytes=64, offset=4 * Q)
+        load_words(vals_window, vals_words)
+
+        query_bf = round_and_interleave("query_bf", query_raw)
+        query_codes = placed.tile([P, Q], U32, name="query_codes", align_bytes=64, offset=0)
+        query_plane = quantise("query_plane", query_codes, query_bf)
+
+        vals_staged = sb.tile([P, I], U8, name="vals_staged", tag="query_bf", align_bytes=64)
+        nc.vector.tensor_copy(vals_staged[:], vals_scale_window[:].indirect(offsets[:]))
+        for r in range(4):
+            nc.sync.dma_start(
+                vals_plane[r:P:32, :].bitcast(I32),
+                vals_staged[STAGE_FIRST + STAGE_STEP * r : P : 32, :].bitcast(I32),
+            )
+
+        turned = ps.tile([P, P], F32, name="turned", tag="bank7")
+        nc.tensor.transpose(turned[:], slot_rows[:], identity[:])
+        steep_neg = sb.tile([P, TILES], F32, name="steep_neg")
+        nc.scalar.activation(steep_neg[:], turned[:, 0:TILES], ACT.Copy, scale=-1.0)
+        gain_neg = sb.tile([P, TILES], F32, name="gain_neg")
+        for t in range(TILES):
+            nc.scalar.activation(gain_neg[:, t : t + 1], turned[:, TILES + t : TILES + t + 1], ACT.Copy, scale=steep_neg[:, t : t + 1])
+        gain_quarter = sb.tile([P, TILES], F32, name="gain_quarter")
+        nc.scalar.activation(gain_quarter[:], gain_neg[:], ACT.Copy, scale=-0.25)
+
+        gout_bf = round_and_interleave("gout_bf", gout_raw)
+
+        keys_picked = sb.tile([P, I], U32, name="keys_picked", tag="vals_scale_window", align_bytes=64)
+        slopes = []
+        for t in range(TILES):
+            part = gather_words(keys_picked, keys_window, t)
+            scores = ps.tile([P, Q], F32, name="scores" + str(t), tag="bank" + str(t))
+            nc.tensor.matmul_mx(
+                out=scores[:], lhsT=part.bitcast(FP8X4), lhsT_scale=keys_plane[:, t * P : (t + 1) * P],
+                rhs=query_codes[:].bitcast(FP8X4), rhs_scale=query_plane[:], start=True, stop=True,
+            )
+            sums = sb.tile([P, G], F32, name="score_sums" + str(t), tag="score_sums" + str(t), align_bytes=64)
+            nc.vector.tensor_reduce(sums[:], by_team(scores[:]), AX.X, ALU.add)
+            centred = sb.tile([P, Q], F32, name="centred" + str(t))
+            nc.vector.scalar_tensor_tensor(by_team(centred[:]), over_team(sums[:]), -1.0 / TEAM, by_team(scores[:]), ALU.mult, ALU.add)
+            weight = sb.tile([P, Q], F32, name="weight" + str(t))
+            nc.scalar.activation(weight[:], centred[:], ACT.Sigmoid, scale=steep_neg[:, t : t + 1])
+            square = sb.tile([P, Q], F32, name="square" + str(t))
+            nc.scalar.activation(square[:], weight[:], ACT.Square, bias=-0.5)
+            slope = sb.tile([P, Q], F32, name="slope" + str(t))
+            nc.scalar.activation(slope[:], square[:], ACT.Identity, scale=gain_neg[:, t : t + 1], bias=gain_quarter[:, t : t + 1])
+            slopes.append(slope)
+
+        gout_codes = sb.tile([P, Q], U32, name="gout_codes", tag="score_sums1", align_bytes=64)
+        gout_plane = quantise("gout_plane", gout_codes, gout_bf)
+        vals_picked = sb.tile([P, I], U32, name="vals_picked", tag="score_sums3", align_bytes=64)
+
+        for t in range(TILES):
+            part = gather_words(vals_picked, vals_window, t)
+            dp = ps.tile([P, Q], F32, name="dp" + str(t), tag="bank" + str(TILES + t))
+            nc.tensor.matmul_mx(
+                out=dp[:], lhsT=part.bitcast(FP8X4), lhsT_scale=vals_plane[:, t * P : (t + 1) * P],
+                rhs=gout_codes[:].bitcast(FP8X4), rhs_scale=gout_plane[:], start=True, stop=True,
+            )
+            dz = sb.tile([P, Q], F32, name="dz" + str(t))
+            nc.vector.tensor_tensor(dz[:], slopes[t][:], dp[:], ALU.mult)
+            sums = sb.tile([P, G], F32, name="dz_sums" + str(t))
+            nc.vector.tensor_reduce(sums[:], by_team(dz[:]), AX.X, ALU.add)
+            result = sb.tile([P, Q], F32, name="result" + str(t))
+            nc.vector.scalar_tensor_tensor(by_team(result[:]), over_team(sums[:]), -1.0 / TEAM, by_team(dz[:]), ALU.mult, ALU.add)
+            nc.sync.dma_start(out[t * P : (t + 1) * P, :], result[:])

@@ -1,7 +1,6 @@
 from contextlib import ExitStack
 
 import concourse.mybir as mybir
-from concourse.masks import make_identity
 
 D, E, T, I, Q, G = 512, 512, 2048, 512, 256, 32
 FLOPS = 2 * I * Q * (D + E)
@@ -23,7 +22,6 @@ TILES = I // P
 TEAM = Q // G
 LIST_COLS = P // 16
 STAGE_STEP = 8
-STAGE_FIRST = 4
 
 
 def tile_attend_gteamcontrast_kernel(tc, query, keys_words, keys_scales, steep, fs, gout, vals_words, vals_scales, offs, out):
@@ -33,41 +31,54 @@ def tile_attend_gteamcontrast_kernel(tc, query, keys_words, keys_scales, steep, 
         placed = ctx.enter_context(tc.tile_pool(name="placed", bufs=1))
         ps = ctx.enter_context(tc.psum_pool(name="ps", bufs=1))
 
+        keys_at = 0
+        gout_at = keys_at + 4 * T
+        vals_at = gout_at + 4 * PACK * Q
+        ramp_at = gout_at - P
+        codes_at = vals_at + 4 * T
+        keys_scales_at = codes_at
+        picked_at = codes_at + 4 * Q
+
         offsets = sb.tile([P, I // 16], U16, name="offsets")
         nc.sync.dma_start(offsets[:], offs)
 
-        def load_rows(name, rows):
-            raw = sb.tile([P, PACK, Q], F32, name=name)
+        def load_rows(raw, rows):
             nc.sync.dma_start(raw[:], rows.rearrange("(p j) q -> p j q", j=PACK))
-            return raw
 
         def load_words(window, words):
             nc.sync.dma_start(window[:].bitcast(I32), words[0].rearrange("p n t -> p (n t)").bitcast(I32))
 
-        keys_scale_window = placed.tile([P, T], U8, name="keys_scale_window", align_bytes=64, offset=0)
+        vals_scale_window = sb.tile([P, T], U8, name="vals_scale_window", align_bytes=64)
+        nc.gpsimd.memset(vals_scale_window[:].bitcast(I32), 0)
+        nc.sync.dma_start(vals_scale_window[0:P:STAGE_STEP, :].bitcast(I32), vals_scales[0].bitcast(I32))
+        keys_scale_window = placed.tile([P, T], U8, name="keys_scale_window", align_bytes=64, offset=keys_scales_at)
         nc.vector.memset(keys_scale_window[:].bitcast(I32), 0)
         for quad in range(4):
-            nc.scalar.dma_start(
+            nc.sync.dma_start(
                 keys_scale_window[32 * quad : 32 * quad + 4, :].bitcast(I32),
                 keys_scales[0, 4 * quad : 4 * quad + 4, :].bitcast(I32),
             )
-        vals_scale_window = sb.tile([P, T], U8, name="vals_scale_window", tag="vals_scale_window", align_bytes=64)
-        nc.vector.memset(vals_scale_window[:].bitcast(I32), 0)
-        nc.scalar.dma_start(vals_scale_window[STAGE_FIRST:P:STAGE_STEP, :].bitcast(I32), vals_scales[0].bitcast(I32))
 
-        query_raw = load_rows("query_raw", query)
-        keys_window = sb.tile([P, T], U32, name="keys_window", align_bytes=64)
+        query_raw = sb.tile([P, PACK, Q], F32, name="query_raw")
+        load_rows(query_raw, query)
+        zeros_area = placed.tile([P, PACK * Q + P // 2], F32, name="zeros_area", align_bytes=64, offset=ramp_at)
+        zeros = zeros_area[:, 0:P]
+        nc.vector.memset(zeros, 0.0)
+        identity = sb.tile([P, P], F32, name="identity")
+        nc.gpsimd.affine_select(
+            out=identity[:], in_=zeros, compare_op=ALU.not_equal, fill=1.0, base=0, pattern=[[-1, P]], channel_multiplier=1
+        )
+        keys_window = placed.tile([P, T], U32, name="keys_window", align_bytes=64, offset=keys_at)
         load_words(keys_window, keys_words)
-        gout_raw = load_rows("gout_raw", gout)
+        gout_raw = placed.tile([P, PACK, Q], F32, name="gout_raw", align_bytes=64, offset=gout_at)
+        load_rows(gout_raw, gout)
+        vals_window = placed.tile([P, T], U32, name="vals_window", align_bytes=64, offset=vals_at)
+        load_words(vals_window, vals_words)
 
         slot_rows = sb.tile([P, P], F32, name="slot_rows", tag="gout_bf", align_bytes=64)
-        nc.gpsimd.memset(slot_rows[:], 0.0)
+        nc.vector.memset(slot_rows[:], 0.0)
         nc.gpsimd.dma_start(slot_rows[0:TILES, :], steep.rearrange("(t p) o -> t (p o)", p=P))
         nc.gpsimd.dma_start(slot_rows[TILES : 2 * TILES, :], fs.rearrange("(t p) o -> t (p o)", p=P))
-        identity = sb.tile([P, P], F32, name="identity")
-        make_identity(nc, identity[:])
-        vals_plane = sb.tile([P, I], U8, name="vals_plane", align_bytes=64)
-        nc.gpsimd.memset(vals_plane[:].bitcast(I32), 0)
 
         def round_and_interleave(name, raw):
             grouped = sb.tile([P, Q * PACK], BF16, name=name, tag=name, align_bytes=64)
@@ -82,82 +93,95 @@ def tile_attend_gteamcontrast_kernel(tc, query, keys_words, keys_scales, steep, 
             nc.vector.quantize_mx(out=codes[:].bitcast(FP8X4), scales=plane[:], in_=grouped[:])
             return plane
 
-        def gather_words(picked, window, t):
-            part = picked[:, t * P : (t + 1) * P]
-            nc.vector.tensor_copy(part, window[:].indirect(offsets[:, t * LIST_COLS : (t + 1) * LIST_COLS]))
-            return part
+        def gather_words(picked, window, first, count):
+            nc.vector.tensor_copy(
+                picked[:, first * P : (first + count) * P],
+                window[:].indirect(offsets[:, first * LIST_COLS : (first + count) * LIST_COLS]),
+            )
+
+        def product(bank, place, picked, plane, t, codes, codes_plane):
+            nc.tensor.matmul_mx(
+                out=bank[:, place * Q : (place + 1) * Q],
+                lhsT=picked[:, t * P : (t + 1) * P].bitcast(FP8X4), lhsT_scale=plane[:, t * P : (t + 1) * P],
+                rhs=codes[:].bitcast(FP8X4), rhs_scale=codes_plane[:], start=True, stop=True,
+            )
 
         def by_team(ap):
             return ap.rearrange("p (g j) -> p g j", j=TEAM)
 
-        def over_team(ap):
-            return ap.unsqueeze(2).to_broadcast([P, G, TEAM])
+        def subtract_team_mean(result, values, sums):
+            teams = sums.shape[1]
+            nc.vector.tensor_reduce(sums, by_team(values), AX.X, ALU.add)
+            nc.vector.scalar_tensor_tensor(
+                by_team(result), sums.unsqueeze(2).to_broadcast([P, teams, TEAM]), -1.0 / TEAM, by_team(values), ALU.mult, ALU.add
+            )
+
+        vals_staged = sb.tile([P, I], U8, name="vals_staged", align_bytes=64)
+        nc.vector.tensor_copy(vals_staged[:], vals_scale_window[:].indirect(offsets[:]))
 
         keys_plane = sb.tile([P, I], U8, name="keys_plane", align_bytes=64)
         nc.vector.tensor_copy(keys_plane[:], keys_scale_window[:].indirect(offsets[:]))
-        vals_window = placed.tile([P, T], U32, name="vals_window", align_bytes=64, offset=4 * Q)
-        load_words(vals_window, vals_words)
-
         query_bf = round_and_interleave("query_bf", query_raw)
-        query_codes = placed.tile([P, Q], U32, name="query_codes", align_bytes=64, offset=0)
+        query_codes = placed.tile([P, Q], U32, name="query_codes", align_bytes=64, offset=codes_at)
         query_plane = quantise("query_plane", query_codes, query_bf)
 
-        vals_staged = sb.tile([P, I], U8, name="vals_staged", tag="query_bf", align_bytes=64)
-        nc.vector.tensor_copy(vals_staged[:], vals_scale_window[:].indirect(offsets[:]))
-        for r in range(4):
-            nc.sync.dma_start(
-                vals_plane[r:P:32, :].bitcast(I32),
-                vals_staged[STAGE_FIRST + STAGE_STEP * r : P : 32, :].bitcast(I32),
-            )
-
-        turned = ps.tile([P, P], F32, name="turned", tag="bank7")
+        turned = ps.tile([P, P], F32, name="turned", tag="turned")
         nc.tensor.transpose(turned[:], slot_rows[:], identity[:])
-        steep_neg = sb.tile([P, TILES], F32, name="steep_neg")
-        nc.scalar.activation(steep_neg[:], turned[:, 0:TILES], ACT.Copy, scale=-1.0)
-        gain_neg = sb.tile([P, TILES], F32, name="gain_neg")
+        steep_half = sb.tile([P, TILES], F32, name="steep_half")
+        nc.scalar.activation(steep_half[:], turned[:, 0:TILES], ACT.Copy, scale=0.5)
+        gain_half = sb.tile([P, TILES], F32, name="gain_half")
         for t in range(TILES):
-            nc.scalar.activation(gain_neg[:, t : t + 1], turned[:, TILES + t : TILES + t + 1], ACT.Copy, scale=steep_neg[:, t : t + 1])
-        gain_quarter = sb.tile([P, TILES], F32, name="gain_quarter")
-        nc.scalar.activation(gain_quarter[:], gain_neg[:], ACT.Copy, scale=-0.25)
+            nc.scalar.activation(gain_half[:, t : t + 1], turned[:, TILES + t : TILES + t + 1], ACT.Copy, scale=steep_half[:, t : t + 1])
+        gain_plus = sb.tile([P, TILES], F32, name="gain_plus")
+        nc.scalar.activation(gain_plus[:], gain_half[:], ACT.Copy, scale=0.5)
+        gain_minus = sb.tile([P, TILES], F32, name="gain_minus")
+        nc.scalar.activation(gain_minus[:], gain_half[:], ACT.Copy, scale=-0.5)
 
         gout_bf = round_and_interleave("gout_bf", gout_raw)
 
-        keys_picked = sb.tile([P, I], U32, name="keys_picked", tag="vals_scale_window", align_bytes=64)
-        slopes = []
-        for t in range(TILES):
-            part = gather_words(keys_picked, keys_window, t)
-            scores = ps.tile([P, Q], F32, name="scores" + str(t), tag="bank" + str(t))
-            nc.tensor.matmul_mx(
-                out=scores[:], lhsT=part.bitcast(FP8X4), lhsT_scale=keys_plane[:, t * P : (t + 1) * P],
-                rhs=query_codes[:].bitcast(FP8X4), rhs_scale=query_plane[:], start=True, stop=True,
-            )
-            sums = sb.tile([P, G], F32, name="score_sums" + str(t), tag="score_sums" + str(t), align_bytes=64)
-            nc.vector.tensor_reduce(sums[:], by_team(scores[:]), AX.X, ALU.add)
-            centred = sb.tile([P, Q], F32, name="centred" + str(t))
-            nc.vector.scalar_tensor_tensor(by_team(centred[:]), over_team(sums[:]), -1.0 / TEAM, by_team(scores[:]), ALU.mult, ALU.add)
-            weight = sb.tile([P, Q], F32, name="weight" + str(t))
-            nc.scalar.activation(weight[:], centred[:], ACT.Sigmoid, scale=steep_neg[:, t : t + 1])
-            square = sb.tile([P, Q], F32, name="square" + str(t))
-            nc.scalar.activation(square[:], weight[:], ACT.Square, bias=-0.5)
-            slope = sb.tile([P, Q], F32, name="slope" + str(t))
-            nc.scalar.activation(slope[:], square[:], ACT.Identity, scale=gain_neg[:, t : t + 1], bias=gain_quarter[:, t : t + 1])
-            slopes.append(slope)
+        keys_picked = placed.tile([P, I], U32, name="keys_picked", align_bytes=64, offset=picked_at)
+        slope = sb.tile([P, TILES * Q], F32, name="slope")
+        for pair in range(2):
+            gather_words(keys_picked, keys_window, 2 * pair, 2)
+            scores = ps.tile([P, 2 * Q], F32, name="scores" + str(pair))
+            for place in range(2):
+                product(scores, place, keys_picked, keys_plane, 2 * pair + place, query_codes, query_plane)
+            sums = sb.tile([P, 2 * G], F32, name="score_sums" + str(pair), tag="score_sums" + str(pair), align_bytes=64)
+            centred = sb.tile([P, 2 * Q], F32, name="centred" + str(pair))
+            subtract_team_mean(centred[:], scores[:], sums[:])
+            tanh = sb.tile([P, 2 * Q], F32, name="tanh" + str(pair))
+            for place in range(2):
+                t = 2 * pair + place
+                nc.scalar.activation(tanh[:, place * Q : (place + 1) * Q], centred[:, place * Q : (place + 1) * Q], ACT.Tanh, scale=steep_half[:, t : t + 1])
+            square = sb.tile([P, 2 * Q], F32, name="square" + str(pair))
+            nc.scalar.activation(square[:], tanh[:], ACT.Square)
+            for place in range(2):
+                t = 2 * pair + place
+                nc.scalar.activation(
+                    slope[:, t * Q : (t + 1) * Q], square[:, place * Q : (place + 1) * Q], ACT.Identity,
+                    scale=gain_minus[:, t : t + 1], bias=gain_plus[:, t : t + 1],
+                )
 
-        gout_codes = sb.tile([P, Q], U32, name="gout_codes", tag="score_sums1", align_bytes=64)
+        vals_plane = placed.tile([P, I], U8, name="vals_plane", align_bytes=64, offset=keys_at)
+        nc.vector.tensor_copy(vals_plane[:].bitcast(I32), vals_staged[:].bitcast(I32))
+        for r in range(1, 4):
+            nc.sync.dma_start(vals_plane[r:P:32, :].bitcast(I32), vals_staged[STAGE_STEP * r : P : 32, :].bitcast(I32))
+
+        gout_codes = sb.tile([P, Q], U32, name="gout_codes", tag="score_sums0", align_bytes=64)
         gout_plane = quantise("gout_plane", gout_codes, gout_bf)
-        vals_picked = sb.tile([P, I], U32, name="vals_picked", tag="score_sums3", align_bytes=64)
+        vals_picked = sb.tile([P, I], U32, name="vals_picked", tag="score_sums1", align_bytes=64)
 
-        for t in range(TILES):
-            part = gather_words(vals_picked, vals_window, t)
-            dp = ps.tile([P, Q], F32, name="dp" + str(t), tag="bank" + str(TILES + t))
-            nc.tensor.matmul_mx(
-                out=dp[:], lhsT=part.bitcast(FP8X4), lhsT_scale=vals_plane[:, t * P : (t + 1) * P],
-                rhs=gout_codes[:].bitcast(FP8X4), rhs_scale=gout_plane[:], start=True, stop=True,
+        for first, count in ((0, 2), (2, 1), (3, 1)):
+            gather_words(vals_picked, vals_window, first, count)
+            dp = ps.tile([P, count * Q], F32, name="dp" + str(first))
+            for place in range(count):
+                product(dp, place, vals_picked, vals_plane, first + place, gout_codes, gout_plane)
+            dz = sb.tile([P, count * Q], F32, name="dz" + str(first))
+            nc.vector.tensor_tensor(dz[:], slope[:, first * Q : (first + count) * Q], dp[:], ALU.mult)
+            sums = sb.tile([P, count * G], F32, name="dz_sums" + str(first))
+            result = sb.tile([P, count * Q], F32, name="result" + str(first))
+            subtract_team_mean(result[:], dz[:], sums[:])
+            nc.sync.dma_start(
+                out[first * P : (first + count) * P, :].rearrange("(t p) q -> p t q", p=P),
+                result[:].rearrange("p (t q) -> p t q", q=Q),
             )
-            dz = sb.tile([P, Q], F32, name="dz" + str(t))
-            nc.vector.tensor_tensor(dz[:], slopes[t][:], dp[:], ALU.mult)
-            sums = sb.tile([P, G], F32, name="dz_sums" + str(t))
-            nc.vector.tensor_reduce(sums[:], by_team(dz[:]), AX.X, ALU.add)
-            result = sb.tile([P, Q], F32, name="result" + str(t))
-            nc.vector.scalar_tensor_tensor(by_team(result[:]), over_team(sums[:]), -1.0 / TEAM, by_team(dz[:]), ALU.mult, ALU.add)
-            nc.sync.dma_start(out[t * P : (t + 1) * P, :], result[:])

@@ -63,22 +63,21 @@ def tile_attend_gteamcontrast_kernel(tc, query, keys_words, keys_scales, steep, 
         load_rows(query_raw, query)
         zeros_area = placed.tile([P, PACK * Q + P // 2], F32, name="zeros_area", align_bytes=64, offset=ramp_at)
         zeros = zeros_area[:, 0:P]
-        nc.vector.memset(zeros, 0.0)
+        nc.gpsimd.memset(zeros, 0.0)
         identity = sb.tile([P, P], F32, name="identity")
         nc.gpsimd.affine_select(
             out=identity[:], in_=zeros, compare_op=ALU.not_equal, fill=1.0, base=0, pattern=[[-1, P]], channel_multiplier=1
         )
+        slot_rows = sb.tile([P, P], F32, name="slot_rows")
+        nc.gpsimd.tensor_copy(slot_rows[:], zeros)
         keys_window = placed.tile([P, T], U32, name="keys_window", align_bytes=64, offset=keys_at)
         load_words(keys_window, keys_words)
+        nc.sync.dma_start(slot_rows[0:TILES, :], steep.rearrange("(t p) o -> t (p o)", p=P))
+        nc.sync.dma_start(slot_rows[TILES : 2 * TILES, :], fs.rearrange("(t p) o -> t (p o)", p=P))
         gout_raw = placed.tile([P, PACK, Q], F32, name="gout_raw", align_bytes=64, offset=gout_at)
         load_rows(gout_raw, gout)
         vals_window = placed.tile([P, T], U32, name="vals_window", align_bytes=64, offset=vals_at)
         load_words(vals_window, vals_words)
-
-        slot_rows = sb.tile([P, P], F32, name="slot_rows", tag="gout_bf", align_bytes=64)
-        nc.vector.memset(slot_rows[:], 0.0)
-        nc.gpsimd.dma_start(slot_rows[0:TILES, :], steep.rearrange("(t p) o -> t (p o)", p=P))
-        nc.gpsimd.dma_start(slot_rows[TILES : 2 * TILES, :], fs.rearrange("(t p) o -> t (p o)", p=P))
 
         def round_and_interleave(name, raw):
             grouped = sb.tile([P, Q * PACK], BF16, name=name, tag=name, align_bytes=64)
@@ -125,38 +124,37 @@ def tile_attend_gteamcontrast_kernel(tc, query, keys_words, keys_scales, steep, 
         query_codes = placed.tile([P, Q], U32, name="query_codes", align_bytes=64, offset=codes_at)
         query_plane = quantise("query_plane", query_codes, query_bf)
 
-        turned = ps.tile([P, P], F32, name="turned", tag="turned")
-        nc.tensor.transpose(turned[:], slot_rows[:], identity[:])
-        steep_half = sb.tile([P, TILES], F32, name="steep_half")
-        nc.scalar.activation(steep_half[:], turned[:, 0:TILES], ACT.Copy, scale=0.5)
-        gain_half = sb.tile([P, TILES], F32, name="gain_half")
-        for t in range(TILES):
-            nc.scalar.activation(gain_half[:, t : t + 1], turned[:, TILES + t : TILES + t + 1], ACT.Copy, scale=steep_half[:, t : t + 1])
-        gain_plus = sb.tile([P, TILES], F32, name="gain_plus")
-        nc.scalar.activation(gain_plus[:], gain_half[:], ACT.Copy, scale=0.5)
-        gain_minus = sb.tile([P, TILES], F32, name="gain_minus")
-        nc.scalar.activation(gain_minus[:], gain_half[:], ACT.Copy, scale=-0.5)
-
         gout_bf = round_and_interleave("gout_bf", gout_raw)
+
+        turned = ps.tile([P, P], F32, name="turned")
+        nc.tensor.transpose(turned[:], slot_rows[:], identity[:])
+        halves = placed.tile([P, 2 * TILES], F32, name="halves", align_bytes=64, offset=gout_at + 4 * Q)
+        nc.scalar.activation(halves[:], turned[:, 0 : 2 * TILES], ACT.Copy, scale=0.5)
+        steep_half = halves[:, 0:TILES]
+        gain_plus = sb.tile([P, TILES], F32, name="gain_plus")
+        for t in range(TILES):
+            nc.scalar.activation(gain_plus[:, t : t + 1], halves[:, TILES + t : TILES + t + 1], ACT.Copy, scale=steep_half[:, t : t + 1])
+        gain_minus = sb.tile([P, TILES], F32, name="gain_minus")
+        nc.scalar.activation(gain_minus[:], gain_plus[:], ACT.Copy, scale=-1.0)
 
         keys_picked = placed.tile([P, I], U32, name="keys_picked", align_bytes=64, offset=picked_at)
         slope = sb.tile([P, TILES * Q], F32, name="slope")
-        for pair in range(2):
-            gather_words(keys_picked, keys_window, 2 * pair, 2)
-            scores = ps.tile([P, 2 * Q], F32, name="scores" + str(pair))
-            for place in range(2):
-                product(scores, place, keys_picked, keys_plane, 2 * pair + place, query_codes, query_plane)
-            sums = sb.tile([P, 2 * G], F32, name="score_sums" + str(pair), tag="score_sums" + str(pair), align_bytes=64)
-            centred = sb.tile([P, 2 * Q], F32, name="centred" + str(pair))
+        for first, count in ((0, 1), (1, 1), (2, 2)):
+            gather_words(keys_picked, keys_window, first, count)
+            scores = ps.tile([P, count * Q], F32, name="scores" + str(first))
+            for place in range(count):
+                product(scores, place, keys_picked, keys_plane, first + place, query_codes, query_plane)
+            sums = sb.tile([P, count * G], F32, name="score_sums" + str(first), tag="score_sums" + str(first), align_bytes=64)
+            centred = sb.tile([P, count * Q], F32, name="centred" + str(first))
             subtract_team_mean(centred[:], scores[:], sums[:])
-            tanh = sb.tile([P, 2 * Q], F32, name="tanh" + str(pair))
-            for place in range(2):
-                t = 2 * pair + place
+            tanh = sb.tile([P, count * Q], F32, name="tanh" + str(first))
+            for place in range(count):
+                t = first + place
                 nc.scalar.activation(tanh[:, place * Q : (place + 1) * Q], centred[:, place * Q : (place + 1) * Q], ACT.Tanh, scale=steep_half[:, t : t + 1])
-            square = sb.tile([P, 2 * Q], F32, name="square" + str(pair))
+            square = sb.tile([P, count * Q], F32, name="square" + str(first))
             nc.scalar.activation(square[:], tanh[:], ACT.Square)
-            for place in range(2):
-                t = 2 * pair + place
+            for place in range(count):
+                t = first + place
                 nc.scalar.activation(
                     slope[:, t * Q : (t + 1) * Q], square[:, place * Q : (place + 1) * Q], ACT.Identity,
                     scale=gain_minus[:, t : t + 1], bias=gain_plus[:, t : t + 1],
@@ -169,10 +167,11 @@ def tile_attend_gteamcontrast_kernel(tc, query, keys_words, keys_scales, steep, 
 
         gout_codes = sb.tile([P, Q], U32, name="gout_codes", tag="score_sums0", align_bytes=64)
         gout_plane = quantise("gout_plane", gout_codes, gout_bf)
-        vals_picked = sb.tile([P, I], U32, name="vals_picked", tag="score_sums1", align_bytes=64)
+        vals_picked = sb.tile([P, I], U32, name="vals_picked", tag="score_sums2", align_bytes=64)
 
         for first, count in ((0, 2), (2, 1), (3, 1)):
-            gather_words(vals_picked, vals_window, first, count)
+            for place in range(count):
+                gather_words(vals_picked, vals_window, first + place, 1)
             dp = ps.tile([P, count * Q], F32, name="dp" + str(first))
             for place in range(count):
                 product(dp, place, vals_picked, vals_plane, first + place, gout_codes, gout_plane)

from contextlib import ExitStack

import concourse.mybir as mybir

D, E, T, I, Q, G = 512, 512, 2048, 512, 256, 32
FLOPS = 2 * I * Q * (D + E)

F32 = mybir.dt.float32
BF16 = mybir.dt.bfloat16
I32 = mybir.dt.int32
U32 = mybir.dt.uint32
U16 = mybir.dt.uint16
U8 = mybir.dt.uint8
FP8X4 = mybir.dt.float8_e4m3fn_x4
ALU = mybir.AluOpType
ACT = mybir.ActivationFunctionType
AX = mybir.AxisListType

P = 128
PACK = 4
TILES = I // P
TEAM = Q // G
LIST_COLS = P // 16
STAGE_STEP = 8


def tile_attend_gteamcontrast_kernel(tc, query, keys_words, keys_scales, steep, fs, gout, vals_words, vals_scales, offs, out):
    nc = tc.nc
    with ExitStack() as ctx:
        sb = ctx.enter_context(tc.tile_pool(name="sb", bufs=1))
        placed = ctx.enter_context(tc.tile_pool(name="placed", bufs=1))
        ps = ctx.enter_context(tc.psum_pool(name="ps", bufs=1))

        keys_at = 0
        gout_at = keys_at + 4 * T
        vals_at = gout_at + 4 * PACK * Q
        ramp_at = gout_at - P
        codes_at = vals_at + 4 * T
        keys_scales_at = codes_at
        picked_at = codes_at + 4 * Q

        offsets = sb.tile([P, I // 16], U16, name="offsets")
        nc.sync.dma_start(offsets[:], offs)

        def load_rows(raw, rows):
            nc.sync.dma_start(raw[:], rows.rearrange("(p j) q -> p j q", j=PACK))

        def load_words(window, words):
            nc.sync.dma_start(window[:].bitcast(I32), words[0].rearrange("p n t -> p (n t)").bitcast(I32))

        vals_scale_window = sb.tile([P, T], U8, name="vals_scale_window", align_bytes=64)
        nc.gpsimd.memset(vals_scale_window[:].bitcast(I32), 0)
        nc.sync.dma_start(vals_scale_window[0:P:STAGE_STEP, :].bitcast(I32), vals_scales[0].bitcast(I32))
        keys_scale_window = placed.tile([P, T], U8, name="keys_scale_window", align_bytes=64, offset=keys_scales_at)
        nc.vector.memset(keys_scale_window[:].bitcast(I32), 0)
        for quad in range(4):
            nc.sync.dma_start(
                keys_scale_window[32 * quad : 32 * quad + 4, :].bitcast(I32),
                keys_scales[0, 4 * quad : 4 * quad + 4, :].bitcast(I32),
            )

        query_raw = sb.tile([P, PACK, Q], F32, name="query_raw")
        load_rows(query_raw, query)
        zeros_area = placed.tile([P, PACK * Q + P // 2], F32, name="zeros_area", align_bytes=64, offset=ramp_at)
        zeros = zeros_area[:, 0:P]
        nc.gpsimd.memset(zeros, 0.0)
        identity = sb.tile([P, P], F32, name="identity")
        nc.gpsimd.affine_select(
            out=identity[:], in_=zeros, compare_op=ALU.not_equal, fill=1.0, base=0, pattern=[[-1, P]], channel_multiplier=1
        )
        slot_rows = sb.tile([P, P], F32, name="slot_rows")
        nc.gpsimd.tensor_copy(slot_rows[:], zeros)
        keys_window = placed.tile([P, T], U32, name="keys_window", align_bytes=64, offset=keys_at)
        load_words(keys_window, keys_words)
        nc.sync.dma_start(slot_rows[0:TILES, :], steep.rearrange("(t p) o -> t (p o)", p=P))
        nc.sync.dma_start(slot_rows[TILES : 2 * TILES, :], fs.rearrange("(t p) o -> t (p o)", p=P))
        gout_raw = placed.tile([P, PACK, Q], F32, name="gout_raw", align_bytes=64, offset=gout_at)
        load_rows(gout_raw, gout)
        vals_window = placed.tile([P, T], U32, name="vals_window", align_bytes=64, offset=vals_at)
        load_words(vals_window, vals_words)

        def round_and_interleave(name, raw):
            grouped = sb.tile([P, Q * PACK], BF16, name=name, tag=name, align_bytes=64)
            nc.scalar.copy(
                grouped[:].rearrange("p (c i j) -> p c j i", i=4, j=PACK),
                raw[:].rearrange("p j (c i) -> p c j i", i=4),
            )
            return grouped

        def quantise(name, codes, grouped):
            plane = sb.tile([P, Q], U8, name=name, align_bytes=64)
            nc.vector.quantize_mx(out=codes[:].bitcast(FP8X4), scales=plane[:], in_=grouped[:])
            return plane

        def gather_words(picked, window, first, count):
            nc.vector.tensor_copy(
                picked[:, first * P : (first + count) * P],
                window[:].indirect(offsets[:, first * LIST_COLS : (first + count) * LIST_COLS]),
            )

        def product(bank, place, picked, plane, t, codes, codes_plane):
            nc.tensor.matmul_mx(
                out=bank[:, place * Q : (place + 1) * Q],
                lhsT=picked[:, t * P : (t + 1) * P].bitcast(FP8X4), lhsT_scale=plane[:, t * P : (t + 1) * P],
                rhs=codes[:].bitcast(FP8X4), rhs_scale=codes_plane[:], start=True, stop=True,
            )

        def by_team(ap):
            return ap.rearrange("p (g j) -> p g j", j=TEAM)

        def subtract_team_mean(result, values, sums):
            teams = sums.shape[1]
            nc.vector.tensor_reduce(sums, by_team(values), AX.X, ALU.add)
            nc.vector.scalar_tensor_tensor(
                by_team(result), sums.unsqueeze(2).to_broadcast([P, teams, TEAM]), -1.0 / TEAM, by_team(values), ALU.mult, ALU.add
            )

        vals_staged = sb.tile([P, I], U8, name="vals_staged", align_bytes=64)
        nc.vector.tensor_copy(vals_staged[:], vals_scale_window[:].indirect(offsets[:]))

        keys_plane = sb.tile([P, I], U8, name="keys_plane", align_bytes=64)
        nc.vector.tensor_copy(keys_plane[:], keys_scale_window[:].indirect(offsets[:]))
        query_bf = round_and_interleave("query_bf", query_raw)
        query_codes = placed.tile([P, Q], U32, name="query_codes", align_bytes=64, offset=codes_at)
        query_plane = quantise("query_plane", query_codes, query_bf)

        gout_bf = round_and_interleave("gout_bf", gout_raw)

        turned = ps.tile([P, P], F32, name="turned")
        nc.tensor.transpose(turned[:], slot_rows[:], identity[:])
        halves = placed.tile([P, 2 * TILES], F32, name="halves", align_bytes=64, offset=gout_at + 4 * Q)
        nc.scalar.activation(halves[:], turned[:, 0 : 2 * TILES], ACT.Copy, scale=0.5)
        steep_half = halves[:, 0:TILES]
        gain_plus = sb.tile([P, TILES], F32, name="gain_plus")
        for t in range(TILES):
            nc.scalar.activation(gain_plus[:, t : t + 1], halves[:, TILES + t : TILES + t + 1], ACT.Copy, scale=steep_half[:, t : t + 1])
        gain_minus = sb.tile([P, TILES], F32, name="gain_minus")
        nc.scalar.activation(gain_minus[:], gain_plus[:], ACT.Copy, scale=-1.0)

        keys_picked = placed.tile([P, I], U32, name="keys_picked", align_bytes=64, offset=picked_at)
        slope = sb.tile([P, TILES * Q], F32, name="slope")
        for first, count in ((0, 1), (1, 1), (2, 2)):
            gather_words(keys_picked, keys_window, first, count)
            scores = ps.tile([P, count * Q], F32, name="scores" + str(first))
            for place in range(count):
                product(scores, place, keys_picked, keys_plane, first + place, query_codes, query_plane)
            sums = sb.tile([P, count * G], F32, name="score_sums" + str(first), tag="score_sums" + str(first), align_bytes=64)
            centred = sb.tile([P, count * Q], F32, name="centred" + str(first))
            subtract_team_mean(centred[:], scores[:], sums[:])
            tanh = sb.tile([P, count * Q], F32, name="tanh" + str(first))
            for place in range(count):
                t = first + place
                nc.scalar.activation(tanh[:, place * Q : (place + 1) * Q], centred[:, place * Q : (place + 1) * Q], ACT.Tanh, scale=steep_half[:, t : t + 1])
            square = sb.tile([P, count * Q], F32, name="square" + str(first))
            nc.scalar.activation(square[:], tanh[:], ACT.Square)
            for place in range(count):
                t = first + place
                nc.scalar.activation(
                    slope[:, t * Q : (t + 1) * Q], square[:, place * Q : (place + 1) * Q], ACT.Identity,
                    scale=gain_minus[:, t : t + 1], bias=gain_plus[:, t : t + 1],
                )

        vals_plane = placed.tile([P, I], U8, name="vals_plane", align_bytes=64, offset=keys_at)
        nc.vector.tensor_copy(vals_plane[:].bitcast(I32), vals_staged[:].bitcast(I32))
        for r in range(1, 4):
            nc.sync.dma_start(vals_plane[r:P:32, :].bitcast(I32), vals_staged[STAGE_STEP * r : P : 32, :].bitcast(I32))

        gout_codes = sb.tile([P, Q], U32, name="gout_codes", tag="score_sums0", align_bytes=64)
        gout_plane = quantise("gout_plane", gout_codes, gout_bf)
        vals_picked = sb.tile([P, I], U32, name="vals_picked", tag="score_sums2", align_bytes=64)

        for first, count in ((0, 2), (2, 1), (3, 1)):
            for place in range(count):
                gather_words(vals_picked, vals_window, first + place, 1)
            dp = ps.tile([P, count * Q], F32, name="dp" + str(first))
            for place in range(count):
                product(dp, place, vals_picked, vals_plane, first + place, gout_codes, gout_plane)
            dz = sb.tile([P, count * Q], F32, name="dz" + str(first))
            nc.vector.tensor_tensor(dz[:], slope[:, first * Q : (first + count) * Q], dp[:], ALU.mult)
            sums = sb.tile([P, count * G], F32, name="dz_sums" + str(first))
            result = sb.tile([P, count * Q], F32, name="result" + str(first))
            subtract_team_mean(result[:], dz[:], sums[:])
            nc.sync.dma_start(
                out[first * P : (first + count) * P, :].rearrange("(t p) q -> p t q", p=P),
                result[:].rearrange("p (t q) -> p t q", q=Q),
            )
